import numpy as np
import ml_dtypes

BF16 = ml_dtypes.bfloat16


def bf(x):
    return np.asarray(x, np.float32).astype(BF16)


def f32(x):
    return np.asarray(x, np.float32)


def f64(x):
    return np.asarray(x).astype(np.float64)


def striped(idx):
    return np.tile(idx.reshape(-1, 16).T, (8, 1))


S, K, M, N, E, Q, V, D = 512, 256, 128, 256, 2, 128, 128, 4


def setup_inputs():
    return {"base": bf(np.random.standard_normal((M, S))), "x": bf(np.random.standard_normal((K, N))), "w": bf(1.5 * np.random.standard_normal((E, K, M)) / np.sqrt(K)), "b": f32(0.5 * np.random.standard_normal((M, 1))), "offs": striped(np.random.permutation(S)[:N])}


def reference(base, x, w, b, offs):
    idx = offs[:16].T.reshape(-1)
    z = f64(base).copy()
    for e in range(E):
        z[:, idx[e * Q : (e + 1) * Q]] += f64(w)[e].T @ f64(x)[:, e * Q : (e + 1) * Q]
    z = np.tanh(z + f64(b))
    return z.reshape(M, V, D).mean(axis=2)

@@ -1,0 +1,61 @@
+import concourse.mybir as mybir
+from concourse.masks import make_identity
+
+BF16, F32, U16 = mybir.dt.bfloat16, mybir.dt.float32, mybir.dt.uint16
+TANH = mybir.ActivationFunctionType.Tanh
+
+M, S = 128, 512
+K, N = 256, 256
+E = 2
+Q = N // E
+D = 4
+V = S // D
+P = 128
+C = K // P
+OFFSETS_PER_COLUMN = 16
+
+FLOPS = 2 * K * M * N
+
+
+def tile_rows_unpool_mean_tanh_kernel(tc, base, x, w, b, offs, out):
+    nc = tc.nc
+    with (
+        tc.tile_pool(name="held", bufs=1) as held,
+        tc.psum_pool(name="psum", bufs=1) as psum,
+    ):
+        base_tile = held.tile([M, S], BF16)
+        nc.sync.dma_start(base_tile[:], base)
+        weights = held.tile([P, E, C, M], BF16)
+        nc.sync.dma_start(weights[:], w.rearrange("e (p c) m -> p e c m", c=C))
+        points = held.tile([P, C, N], BF16)
+        nc.sync.dma_start(points[:], x.rearrange("(p c) n -> p c n", c=C))
+        offsets = held.tile([P, N // OFFSETS_PER_COLUMN], U16)
+        nc.sync.dma_start(offsets[:], offs)
+        bias = held.tile([M, 1], F32)
+        nc.sync.dma_start(bias[:], b)
+
+        zeros = held.tile([P, 1], F32)
+        nc.vector.memset(zeros[:], 0.0)
+        table_load = held.tile([P, 1], F32)
+        nc.scalar.activation(table_load[:], zeros[:], TANH)
+
+        identity = held.tile([P, P], BF16)
+        make_identity(nc, identity[:])
+
+        window = psum.tile([M, S], F32)
+        nc.tensor.matmul(window[:], identity[:], base_tile[:], start=True, stop=False)
+
+        piece_columns = Q // OFFSETS_PER_COLUMN
+        for e in range(E):
+            cells = window[:].indirect(offsets[:, e * piece_columns : (e + 1) * piece_columns])
+            for c in range(C):
+                last = e == E - 1 and c == C - 1
+                nc.tensor.matmul(cells, weights[:, e, c, :], points[:, c, e * Q : (e + 1) * Q], start=False, stop=last)
+
+        t = held.tile([M, V, D], F32)
+        nc.scalar.activation(t[:].rearrange("m v d -> m (v d)"), window[:], TANH, bias=bias[:])
+        sums = held.tile([M, V], F32)
+        nc.vector.tensor_reduce(sums[:], t[:], mybir.AxisListType.X, mybir.AluOpType.add)
+        means = held.tile([M, V], F32)
+        nc.vector.tensor_scalar_mul(means[:], sums[:], 1.0 / D)
+        nc.sync.dma_start(out, means[:])

@@ -12,6 +12,8 @@ D = 4
 V = S // D
 P = 128
 C = K // P
+CHUNKS = 4
+WARM_UPS = 12
 OFFSETS_PER_COLUMN = 16
 
 FLOPS = 2 * K * M * N
@@ -34,10 +36,15 @@ def tile_rows_unpool_mean_tanh_kernel(tc, base, x, w, b, offs, out):
         bias = held.tile([M, 1], F32)
         nc.sync.dma_start(bias[:], b)
 
-        zeros = held.tile([P, 1], F32)
+        zeros = held.tile([P, P], BF16)
         nc.vector.memset(zeros[:], 0.0)
+
+        unread = psum.tile([P, P], F32)
+        for turn in range(WARM_UPS):
+            nc.tensor.matmul(unread[:], zeros[:], zeros[:], start=True, stop=True)
+
         table_load = held.tile([P, 1], F32)
-        nc.scalar.activation(table_load[:], zeros[:], TANH)
+        nc.scalar.activation(table_load[:], zeros[:, :1], TANH)
 
         identity = held.tile([P, P], BF16)
         make_identity(nc, identity[:])
@@ -53,9 +60,15 @@ def tile_rows_unpool_mean_tanh_kernel(tc, base, x, w, b, offs, out):
                 nc.tensor.matmul(cells, weights[:, e, c, :], points[:, c, e * Q : (e + 1) * Q], start=False, stop=last)
 
         t = held.tile([M, V, D], F32)
-        nc.scalar.activation(t[:].rearrange("m v d -> m (v d)"), window[:], TANH, bias=bias[:])
         sums = held.tile([M, V], F32)
-        nc.vector.tensor_reduce(sums[:], t[:], mybir.AxisListType.X, mybir.AluOpType.add)
+        run = V // CHUNKS
+        for chunk in range(CHUNKS):
+            pooled = slice(chunk * run, (chunk + 1) * run)
+            cells_of_run = slice(chunk * run * D, (chunk + 1) * run * D)
+            nc.scalar.activation(
+                t[:, pooled, :].rearrange("m v d -> m (v d)"), window[:, cells_of_run], TANH, bias=bias[:]
+            )
+            nc.vector.tensor_reduce(sums[:, pooled], t[:, pooled, :], mybir.AxisListType.X, mybir.AluOpType.add)
         means = held.tile([M, V], F32)
         nc.vector.tensor_scalar_mul(means[:], sums[:], 1.0 / D)
         nc.sync.dma_start(out, means[:])

import concourse.mybir as mybir
from concourse.masks import make_identity

BF16, F32, U16 = mybir.dt.bfloat16, mybir.dt.float32, mybir.dt.uint16
TANH = mybir.ActivationFunctionType.Tanh

M, S = 128, 512
K, N = 256, 256
E = 2
Q = N // E
D = 4
V = S // D
P = 128
C = K // P
CHUNKS = 4
WARM_UPS = 12
OFFSETS_PER_COLUMN = 16

FLOPS = 2 * K * M * N


def tile_rows_unpool_mean_tanh_kernel(tc, base, x, w, b, offs, out):
    nc = tc.nc
    with (
        tc.tile_pool(name="held", bufs=1) as held,
        tc.psum_pool(name="psum", bufs=1) as psum,
    ):
        base_tile = held.tile([M, S], BF16)
        nc.sync.dma_start(base_tile[:], base)
        weights = held.tile([P, E, C, M], BF16)
        nc.sync.dma_start(weights[:], w.rearrange("e (p c) m -> p e c m", c=C))
        points = held.tile([P, C, N], BF16)
        nc.sync.dma_start(points[:], x.rearrange("(p c) n -> p c n", c=C))
        offsets = held.tile([P, N // OFFSETS_PER_COLUMN], U16)
        nc.sync.dma_start(offsets[:], offs)
        bias = held.tile([M, 1], F32)
        nc.sync.dma_start(bias[:], b)

        zeros = held.tile([P, P], BF16)
        nc.vector.memset(zeros[:], 0.0)

        unread = psum.tile([P, P], F32)
        for turn in range(WARM_UPS):
            nc.tensor.matmul(unread[:], zeros[:], zeros[:], start=True, stop=True)

        table_load = held.tile([P, 1], F32)
        nc.scalar.activation(table_load[:], zeros[:, :1], TANH)

        identity = held.tile([P, P], BF16)
        make_identity(nc, identity[:])

        window = psum.tile([M, S], F32)
        nc.tensor.matmul(window[:], identity[:], base_tile[:], start=True, stop=False)

        piece_columns = Q // OFFSETS_PER_COLUMN
        for e in range(E):
            cells = window[:].indirect(offsets[:, e * piece_columns : (e + 1) * piece_columns])
            for c in range(C):
                last = e == E - 1 and c == C - 1
                nc.tensor.matmul(cells, weights[:, e, c, :], points[:, c, e * Q : (e + 1) * Q], start=False, stop=last)

        t = held.tile([M, V, D], F32)
        sums = held.tile([M, V], F32)
        run = V // CHUNKS
        for chunk in range(CHUNKS):
            pooled = slice(chunk * run, (chunk + 1) * run)
            cells_of_run = slice(chunk * run * D, (chunk + 1) * run * D)
            nc.scalar.activation(
                t[:, pooled, :].rearrange("m v d -> m (v d)"), window[:, cells_of_run], TANH, bias=bias[:]
            )
            nc.vector.tensor_reduce(sums[:, pooled], t[:, pooled, :], mybir.AxisListType.X, mybir.AluOpType.add)
        means = held.tile([M, V], F32)
        nc.vector.tensor_scalar_mul(means[:], sums[:], 1.0 / D)
        nc.sync.dma_start(out, means[:])
